import numpy as np
import ml_dtypes

BF16 = ml_dtypes.bfloat16


def bf(x):
    return np.asarray(x, np.float32).astype(BF16)


def f32(x):
    return np.asarray(x, np.float32)


def f64(x):
    return np.asarray(x).astype(np.float64)


def striped(idx):
    return np.tile(idx.reshape(-1, 16).T, (8, 1))


S, K, M, N, B, Q = 512, 128, 128, 256, 4, 64


def setup_inputs():
    return {"base": bf(np.random.standard_normal((B, M, S))), "x": bf(np.random.standard_normal((K, N))), "w": bf(np.random.standard_normal((K, M)) / np.sqrt(K)), "c": f32(0.2 + 0.8 * np.random.random_sample((1, S))), "offs": striped(np.random.permutation(S)[:N])}


def reference(base, x, w, c, offs):
    idx = offs[:16].T.reshape(-1)
    z = f64(base).copy()
    for i in range(B):
        z[i][:, idx[i * Q : (i + 1) * Q]] = f64(w).T @ f64(x)[:, i * Q : (i + 1) * Q]
    return z * f64(c)

@@ -1,0 +1,58 @@
+import concourse.mybir as mybir
+from concourse.masks import make_identity
+
+BF16, F32, U16 = mybir.dt.bfloat16, mybir.dt.float32, mybir.dt.uint16
+MULT = mybir.AluOpType.mult
+
+B, M, S = 4, 128, 512
+K, N = 128, 256
+Q = N // B
+OFFSETS_A_COLUMN = 16
+
+FLOPS = 2 * K * M * N + B * M * S
+
+
+def tile_scatter_matmul_kernel(tc, base, x, w, c, offs, out):
+    nc = tc.nc
+    with (
+        tc.tile_pool(name="held", bufs=1) as held,
+        tc.psum_pool(name="psum", bufs=1) as psum,
+    ):
+        offsets = held.tile([128, N // OFFSETS_A_COLUMN], U16, name="offsets")
+        base_tiles = [held.tile([M, S], BF16, name=f"base{i}") for i in range(B)]
+        weights = held.tile([K, M], BF16, name="weights")
+        moving = held.tile([K, N], BF16, name="moving")
+        c_row = held.tile([1, S], F32, name="c_row")
+
+        nc.sync.dma_start(c_row[:], c)
+        for i in range(B):
+            nc.sync.dma_start(base_tiles[i][:], base[i])
+        nc.sync.dma_start(weights[:], w)
+        nc.sync.dma_start(moving[:], x)
+        nc.sync.dma_start(offsets[:], offs)
+
+        ones = held.tile([1, M], F32, name="ones")
+        nc.vector.memset(ones[:], 1.0)
+        identity = held.tile([M, M], BF16, name="identity")
+        make_identity(nc, identity[:])
+
+        c_bank = psum.tile([M, S], F32, name="c_bank")
+        nc.tensor.matmul(c_bank[:], ones[:], c_row[:], start=True, stop=True)
+        c_all = held.tile([M, S], F32, name="c_all")
+        nc.vector.tensor_copy(c_all[:], c_bank[:])
+
+        windows = [psum.tile([M, S], F32, name=f"window{i}") for i in range(B)]
+        for i in range(B):
+            nc.tensor.matmul(windows[i][:], identity[:], base_tiles[i][:], start=True, stop=True)
+
+        columns = Q // OFFSETS_A_COLUMN
+        for i in range(B):
+            piece = offsets[:, i * columns : (i + 1) * columns]
+            nc.tensor.matmul(
+                windows[i][:].indirect(piece), weights[:], moving[:, i * Q : (i + 1) * Q], start=True, stop=True
+            )
+
+        for i in range(B):
+            scaled = held.tile([M, S], F32, name=f"scaled{i}")
+            nc.vector.tensor_tensor(scaled[:], windows[i][:], c_all[:], MULT)
+            nc.sync.dma_start(out[i], scaled[:])

@@ -22,24 +22,17 @@ def tile_scatter_matmul_kernel(tc, base, x, w, c, offs, out):
         base_tiles = [held.tile([M, S], BF16, name=f"base{i}") for i in range(B)]
         weights = held.tile([K, M], BF16, name="weights")
         moving = held.tile([K, N], BF16, name="moving")
-        c_row = held.tile([1, S], F32, name="c_row")
+        c_all = held.tile([M, S], F32, name="c_all")
 
-        nc.sync.dma_start(c_row[:], c)
         for i in range(B):
             nc.sync.dma_start(base_tiles[i][:], base[i])
         nc.sync.dma_start(weights[:], w)
         nc.sync.dma_start(moving[:], x)
         nc.sync.dma_start(offsets[:], offs)
+        nc.sync.dma_start(c_all[:], c.rearrange("o t -> (o t)").partition_broadcast(M))
 
-        ones = held.tile([1, M], F32, name="ones")
-        nc.vector.memset(ones[:], 1.0)
         identity = held.tile([M, M], BF16, name="identity")
         make_identity(nc, identity[:])
-
-        c_bank = psum.tile([M, S], F32, name="c_bank")
-        nc.tensor.matmul(c_bank[:], ones[:], c_row[:], start=True, stop=True)
-        c_all = held.tile([M, S], F32, name="c_all")
-        nc.vector.tensor_copy(c_all[:], c_bank[:])
 
         windows = [psum.tile([M, S], F32, name=f"window{i}") for i in range(B)]
         for i in range(B):

@@ -8,6 +8,7 @@ B, M, S = 4, 128, 512
 K, N = 128, 256
 Q = N // B
 OFFSETS_A_COLUMN = 16
+WARM_UPS = 4
 
 FLOPS = 2 * K * M * N + B * M * S
 
@@ -19,13 +20,14 @@ def tile_scatter_matmul_kernel(tc, base, x, w, c, offs, out):
         tc.psum_pool(name="psum", bufs=1) as psum,
     ):
         offsets = held.tile([128, N // OFFSETS_A_COLUMN], U16, name="offsets")
-        base_tiles = [held.tile([M, S], BF16, name=f"base{i}") for i in range(B)]
+        base_halves = [held.tile([M, B // 2, S], BF16, name=f"base_half{h}") for h in range(2)]
         weights = held.tile([K, M], BF16, name="weights")
         moving = held.tile([K, N], BF16, name="moving")
         c_all = held.tile([M, S], F32, name="c_all")
 
-        for i in range(B):
-            nc.sync.dma_start(base_tiles[i][:], base[i])
+        for h in range(2):
+            first = h * (B // 2)
+            nc.sync.dma_start(base_halves[h][:], base[first : first + B // 2].rearrange("b m s -> m b s"))
         nc.sync.dma_start(weights[:], w)
         nc.sync.dma_start(moving[:], x)
         nc.sync.dma_start(offsets[:], offs)
@@ -34,9 +36,16 @@ def tile_scatter_matmul_kernel(tc, base, x, w, c, offs, out):
         identity = held.tile([M, M], BF16, name="identity")
         make_identity(nc, identity[:])
 
+        zeros = held.tile([K, S], BF16, name="zeros")
+        nc.vector.memset(zeros[:], 0.0)
+        spare = psum.tile([M, S], F32, name="spare")
+        for warm_up in range(WARM_UPS):
+            nc.tensor.matmul(spare[:], zeros[:, :M], zeros[:], start=True, stop=True)
+
         windows = [psum.tile([M, S], F32, name=f"window{i}") for i in range(B)]
         for i in range(B):
-            nc.tensor.matmul(windows[i][:], identity[:], base_tiles[i][:], start=True, stop=True)
+            held_base = base_halves[i // (B // 2)][:, i % (B // 2), :]
+            nc.tensor.matmul(windows[i][:], identity[:], held_base, start=True, stop=True)
 
         columns = Q // OFFSETS_A_COLUMN
         for i in range(B):

@@ -8,7 +8,7 @@ B, M, S = 4, 128, 512
 K, N = 128, 256
 Q = N // B
 OFFSETS_A_COLUMN = 16
-WARM_UPS = 4
+WARM_UPS = 2
 
 FLOPS = 2 * K * M * N + B * M * S
 
@@ -23,16 +23,18 @@ def tile_scatter_matmul_kernel(tc, base, x, w, c, offs, out):
         base_halves = [held.tile([M, B // 2, S], BF16, name=f"base_half{h}") for h in range(2)]
         weights = held.tile([K, M], BF16, name="weights")
         moving = held.tile([K, N], BF16, name="moving")
-        c_all = held.tile([M, S], F32, name="c_all")
+        c_row = held.tile([1, S], F32, name="c_row")
 
+        nc.sync.dma_start(c_row[:], c)
         for h in range(2):
             first = h * (B // 2)
             nc.sync.dma_start(base_halves[h][:], base[first : first + B // 2].rearrange("b m s -> m b s"))
         nc.sync.dma_start(weights[:], w)
         nc.sync.dma_start(moving[:], x)
         nc.sync.dma_start(offsets[:], offs)
-        nc.sync.dma_start(c_all[:], c.rearrange("o t -> (o t)").partition_broadcast(M))
 
+        ones = held.tile([1, M], F32, name="ones")
+        nc.vector.memset(ones[:], 1.0)
         identity = held.tile([M, M], BF16, name="identity")
         make_identity(nc, identity[:])
 
@@ -41,6 +43,11 @@ def tile_scatter_matmul_kernel(tc, base, x, w, c, offs, out):
         spare = psum.tile([M, S], F32, name="spare")
         for warm_up in range(WARM_UPS):
             nc.tensor.matmul(spare[:], zeros[:, :M], zeros[:], start=True, stop=True)
+
+        c_bank = psum.tile([M, S], F32, name="c_bank")
+        nc.tensor.matmul(c_bank[:], ones[:], c_row[:], start=True, stop=True)
+        c_all = held.tile([M, S], F32, name="c_all")
+        nc.vector.tensor_copy(c_all[:], c_bank[:])
 
         windows = [psum.tile([M, S], F32, name=f"window{i}") for i in range(B)]
         for i in range(B):

@@ -8,7 +8,7 @@ B, M, S = 4, 128, 512
 K, N = 128, 256
 Q = N // B
 OFFSETS_A_COLUMN = 16
-WARM_UPS = 2
+WARM_UPS = 4
 
 FLOPS = 2 * K * M * N + B * M * S
 
@@ -33,16 +33,18 @@ def tile_scatter_matmul_kernel(tc, base, x, w, c, offs, out):
         nc.sync.dma_start(moving[:], x)
         nc.sync.dma_start(offsets[:], offs)
 
-        ones = held.tile([1, M], F32, name="ones")
-        nc.vector.memset(ones[:], 1.0)
+        zeros = held.tile([K, M], BF16, name="zeros")
+        nc.gpsimd.memset(zeros[:], 0.0)
+        blocks = S // M
+        spare = psum.tile([M, blocks, M], F32, name="spare")
+        for warm_up in range(WARM_UPS):
+            repeated = zeros[:].unsqueeze(1).to_broadcast([K, blocks, M])
+            nc.tensor.matmul(spare[:], zeros[:], repeated, start=True, stop=True)
+
         identity = held.tile([M, M], BF16, name="identity")
         make_identity(nc, identity[:])
-
-        zeros = held.tile([K, S], BF16, name="zeros")
-        nc.vector.memset(zeros[:], 0.0)
-        spare = psum.tile([M, S], F32, name="spare")
-        for warm_up in range(WARM_UPS):
-            nc.tensor.matmul(spare[:], zeros[:, :M], zeros[:], start=True, stop=True)
+        ones = held.tile([1, M], F32, name="ones")
+        nc.vector.memset(ones[:], 1.0)
 
         c_bank = psum.tile([M, S], F32, name="c_bank")
         nc.tensor.matmul(c_bank[:], ones[:], c_row[:], start=True, stop=True)

import concourse.mybir as mybir
from concourse.masks import make_identity

BF16, F32, U16 = mybir.dt.bfloat16, mybir.dt.float32, mybir.dt.uint16
MULT = mybir.AluOpType.mult

B, M, S = 4, 128, 512
K, N = 128, 256
Q = N // B
OFFSETS_A_COLUMN = 16
WARM_UPS = 4

FLOPS = 2 * K * M * N + B * M * S


def tile_scatter_matmul_kernel(tc, base, x, w, c, offs, out):
    nc = tc.nc
    with (
        tc.tile_pool(name="held", bufs=1) as held,
        tc.psum_pool(name="psum", bufs=1) as psum,
    ):
        offsets = held.tile([128, N // OFFSETS_A_COLUMN], U16, name="offsets")
        base_halves = [held.tile([M, B // 2, S], BF16, name=f"base_half{h}") for h in range(2)]
        weights = held.tile([K, M], BF16, name="weights")
        moving = held.tile([K, N], BF16, name="moving")
        c_row = held.tile([1, S], F32, name="c_row")

        nc.sync.dma_start(c_row[:], c)
        for h in range(2):
            first = h * (B // 2)
            nc.sync.dma_start(base_halves[h][:], base[first : first + B // 2].rearrange("b m s -> m b s"))
        nc.sync.dma_start(weights[:], w)
        nc.sync.dma_start(moving[:], x)
        nc.sync.dma_start(offsets[:], offs)

        zeros = held.tile([K, M], BF16, name="zeros")
        nc.gpsimd.memset(zeros[:], 0.0)
        blocks = S // M
        spare = psum.tile([M, blocks, M], F32, name="spare")
        for warm_up in range(WARM_UPS):
            repeated = zeros[:].unsqueeze(1).to_broadcast([K, blocks, M])
            nc.tensor.matmul(spare[:], zeros[:], repeated, start=True, stop=True)

        identity = held.tile([M, M], BF16, name="identity")
        make_identity(nc, identity[:])
        ones = held.tile([1, M], F32, name="ones")
        nc.vector.memset(ones[:], 1.0)

        c_bank = psum.tile([M, S], F32, name="c_bank")
        nc.tensor.matmul(c_bank[:], ones[:], c_row[:], start=True, stop=True)
        c_all = held.tile([M, S], F32, name="c_all")
        nc.vector.tensor_copy(c_all[:], c_bank[:])

        windows = [psum.tile([M, S], F32, name=f"window{i}") for i in range(B)]
        for i in range(B):
            held_base = base_halves[i // (B // 2)][:, i % (B // 2), :]
            nc.tensor.matmul(windows[i][:], identity[:], held_base, start=True, stop=True)

        columns = Q // OFFSETS_A_COLUMN
        for i in range(B):
            piece = offsets[:, i * columns : (i + 1) * columns]
            nc.tensor.matmul(
                windows[i][:].indirect(piece), weights[:], moving[:, i * Q : (i + 1) * Q], start=True, stop=True
            )

        for i in range(B):
            scaled = held.tile([M, S], F32, name=f"scaled{i}")
            nc.vector.tensor_tensor(scaled[:], windows[i][:], c_all[:], MULT)
            nc.sync.dma_start(out[i], scaled[:])
